import numpy as np
import ml_dtypes


def mxq(x, axis, fmt="e4m3"):
    dtype, down = {"e4m3": (ml_dtypes.float8_e4m3fn, 7), "e5m2": (ml_dtypes.float8_e5m2, 14)}[fmt]
    v = np.moveaxis(np.asarray(x, np.float32).astype(ml_dtypes.bfloat16).astype(np.float64), axis, -1)
    blocks = v.reshape(v.shape[:-1] + (-1, 32))
    amax = np.abs(blocks).max(-1, keepdims=True)
    byte = np.maximum(np.where(amax > 0, np.frexp(amax)[1] - 1 + 127, 0) - down, 1)
    scale = np.exp2(byte - 127.0)
    codes = (blocks / scale).astype(np.float32).astype(dtype).astype(np.float64)
    return np.moveaxis((codes * scale).reshape(v.shape), -1, axis)


WIDE = False


def mx_kscale(k):
    if not WIDE:
        return np.ones(k)
    levels = np.array([10, -10, 5, -5, 0])
    if k % 512:
        return np.exp2(np.random.permutation(np.resize(levels, k // 32))).repeat(32)
    a = np.empty((k // 512, 16))
    for p in range(k // 512):
        a[p, :8] = np.random.permutation(np.resize(levels, 8))
        for g in range(8):
            far = levels[np.abs(levels - a[p, g]) >= 10]
            a[p, g + 8] = far[np.random.randint(len(far))]
    return np.exp2(a.ravel()).repeat(32)


def f64(x):
    return np.asarray(x).astype(np.float64)


def striped(idx):
    return np.tile(idx.reshape(-1, 16).T, (8, 1)).astype(np.uint16)


def unstriped(offs):
    return offs[:16].T.reshape(-1).astype(np.int64)


E2M1 = np.array([0.0, 0.5, 1.0, 1.5, 2.0, 3.0, 4.0, 6.0, -0.0, -0.5, -1.0, -1.5, -2.0, -3.0, -4.0, -6.0])


def pack_weight(w, fmt):
    k, n = w.shape
    w = f64(np.asarray(w, np.float32).astype(ml_dtypes.bfloat16)).reshape(k // 32, 32, n)
    amax = np.abs(w).max(1)
    if fmt == "e4m3":
        byte = np.frexp(amax)[1] - 1 + 127 - 7
    else:
        mant, ex = np.frexp(amax / 6.0)
        byte = np.where(mant > 0.5, ex, ex - 1) + 127
    byte = np.clip(np.where(amax > 0, byte, 1), 1, 254)
    scaled = (w * np.exp2(127.0 - byte)[:, None, :]).reshape(k, n).astype(np.float32)
    by_word = np.ascontiguousarray(scaled.reshape(k // 512, 128, 4, n).transpose(0, 1, 3, 2))
    if fmt == "e4m3":
        words = by_word.astype(ml_dtypes.float8_e4m3fn).view(np.uint8)
    else:
        c = by_word.astype(ml_dtypes.float4_e2m1fn).view(np.uint8) & 0xF
        words = (c[..., 0::2] | (c[..., 1::2] << 4)).reshape(k // 512, 128, 2 * n)
    return np.ascontiguousarray(words), np.ascontiguousarray(byte.astype(np.uint8).reshape(k // 512, 16, n))


def unpack_weight(words, scales, fmt):
    g, _, n = scales.shape
    words = np.ascontiguousarray(words).reshape(g, 128, n, -1)
    if fmt == "e4m3":
        vals = words.view(ml_dtypes.float8_e4m3fn).astype(np.float64)
    else:
        nib = np.empty((g, 128, n, 4), np.uint8)
        nib[..., 0::2] = words & 0xF
        nib[..., 1::2] = words >> 4
        vals = E2M1[nib]
    vals = vals * np.repeat(np.exp2(scales.astype(np.float64) - 127.0), 8, axis=1)[..., None]
    return vals.transpose(0, 1, 3, 2).reshape(g * 512, n)


def gelu(v):
    return 0.5 * v * (1.0 + np.tanh(np.sqrt(2.0 / np.pi) * (v + 0.044715 * v**3)))


K, H, T, S, T2, P, L = 1024, 1024, 2048, 512, 1024, 512, 128

def setup_inputs():
    n = np.random.standard_normal
    s = mx_kscale(K)[:, None]
    u = mx_kscale(H)[:, None]
    d = {}
    d["tab_words"], d["tab_scales"] = pack_weight(n((K, T)) * s, "e4m3")
    d["offs"] = striped(np.random.permutation(T)[:S])
    d["w1"] = (1.2 * n((K, H)) / K ** 0.5 / s).astype(np.float32)
    d["site"] = (0.8 * n((H, S))).astype(np.float32)
    d["w4_words"], d["w4_scales"] = pack_weight(n((K, H)) / K ** 0.5 / s, "e2m1")
    d["page0"] = (1.4 * n((H, T2))).astype(np.float32)
    d["wgs"] = np.exp(0.3 * n((L, S))).astype(np.float32)
    d["offs2"] = striped(np.random.permutation(T2)[:S])
    d["offs3"] = striped(np.random.permutation(T2)[:P])
    d["offs4"] = striped(np.random.permutation(T2)[:P])
    d["gain"] = (np.exp(0.3 * n(H)) * u[:, 0]).astype(np.float32)
    d["w3"] = (1.9 * n((H, H)) / H ** 0.5 / u).astype(np.float32)
    d["stack"] = np.exp(0.3 * n(H)).astype(np.float32)
    d["limit"] = (1.2 * n((H, P))).astype(np.float32)
    return d

def reference(tab_words, tab_scales, offs, w1, site, w4_words, w4_scales, page0, wgs, offs2, offs3, offs4, gain, w3, stack, limit):
    v = unpack_weight(tab_words, tab_scales, "e4m3")[:, unstriped(offs)]
    w4 = unpack_weight(w4_words, w4_scales, "e2m1")
    f = (mxq(f64(w1), 0, "e4m3").T @ v) + f64(site)
    f = 0.5 * f * (1.0 + np.tanh(0.7978845608 * (f + 0.044715 * f ** 3)))
    h = f + (w4.T @ v)
    page = f64(page0).copy()
    page[:, unstriped(offs2)] = np.tile(f64(wgs), (H // L, 1)) * h
    x = np.tanh(page[:, unstriped(offs3)]) * f64(gain)[:, None]
    y = mxq(f64(w3), 0, "e4m3").T @ mxq(x, 0, "e4m3")
    shared = page[:, unstriped(offs4)] * f64(stack)[:, None]
    return np.maximum(y, shared) + np.minimum(y, f64(limit))

@@ -1,0 +1,252 @@
+from contextlib import ExitStack
+
+import concourse.mybir as mybir
+from concourse.masks import make_identity
+
+K, H, T, S, T2, PICK = 1024, 1024, 2048, 512, 1024, 512
+FLOPS = 3 * 2 * 1024 * 1024 * 512
+
+F32 = mybir.dt.float32
+BF16 = mybir.dt.bfloat16
+I32 = mybir.dt.int32
+U32 = mybir.dt.uint32
+U16 = mybir.dt.uint16
+U8 = mybir.dt.uint8
+FP8X4 = mybir.dt.float8_e4m3fn_x4
+FP4X4 = mybir.dt.float4_e2m1fn_x4
+ALU = mybir.AluOpType
+ACT = mybir.ActivationFunctionType
+
+P = 128
+PACK = 4
+PASS_K = P * PACK
+PASSES = K // PASS_K
+TILES = H // P
+TILES_PER_PASS = PASS_K // P
+
+
+def tile_list_flue_register_review_kernel(
+    tc, tab_words, tab_scales, offs, w1, site, w4_words, w4_scales, page0, wgs,
+    offs2, offs3, offs4, gain, w3, stack, limit, out,
+):
+    nc = tc.nc
+    with ExitStack() as ctx:
+        lists = ctx.enter_context(tc.tile_pool(name="lists", bufs=1))
+        keep = ctx.enter_context(tc.tile_pool(name="keep", bufs=1))
+        work = ctx.enter_context(tc.tile_pool(name="work", bufs=2))
+        psum = ctx.enter_context(tc.psum_pool(name="psum", bufs=1))
+
+        idx = lists.tile([P, S // 16], U16, name="idx")
+        idx2 = lists.tile([P, S // 16], U16, name="idx2")
+        idx3 = lists.tile([P, PICK // 16], U16, name="idx3")
+        idx4 = lists.tile([P, PICK // 16], U16, name="idx4")
+
+        tabw = [keep.tile([P, T], I32, name=f"tabw{a}") for a in range(PASSES)]
+        tabs = keep.tile([P, PASSES, T], U8, name="tabs")
+        vw = [keep.tile([P, S], U32, name=f"vw{a}", align_bytes=64) for a in range(PASSES)]
+        vs = [keep.tile([P, S], U8, name=f"vs{a}", align_bytes=64) for a in range(PASSES)]
+        w4w = keep.tile([P, PASSES, 2 * H], U8, name="w4w", align_bytes=64)
+        w4s = keep.tile([P, PASSES, H], U8, name="w4s", align_bytes=64)
+        site_t = [keep.tile([P, S], F32, name=f"site{c}", tag=f"site{c}", align_bytes=64) for c in range(TILES)]
+        page = [keep.tile([P, T2], F32, name=f"page{c}", tag=f"page{c}", align_bytes=64) for c in range(TILES)]
+        lim = [keep.tile([P, PICK], F32, name=f"lim{c}") for c in range(TILES)]
+        wgs_t = keep.tile([P, S], F32, name="wgs_t")
+        gain_t = keep.tile([P, TILES], F32, name="gain_t")
+        stack_t = keep.tile([P, TILES], F32, name="stack_t")
+        ident_b = keep.tile([P, P], BF16, name="ident_b")
+        ident_f = keep.tile([P, P], F32, name="ident_f")
+
+        raw = {}
+        quant = {}
+
+        def load_weight(which, w, col0, width, a):
+            t = work.tile([P, PACK, width], F32, name=f"raw{which}_{col0}_{a}", tag="raw", bufs=8)
+            rows = w[a * PASS_K : (a + 1) * PASS_K, col0 : col0 + width]
+            nc.sync.dma_start(out=t[:], in_=rows.rearrange("(p t) c -> p t c", t=PACK))
+            raw[(which, col0, a)] = t
+
+        def quantize_weight(which, col0, width, tag, on_vector=False):
+            codes = keep.tile([P, PASSES, width], U32, name=f"codes{which}_{col0}", tag=tag, align_bytes=64)
+            for a in range(PASSES):
+                quantize_pass(which, col0, width, a, codes[:, a, :], on_vector)
+
+        def quantize_pass(which, col0, width, a, codes, on_vector):
+            grouped = work.tile([P, width, PACK], BF16, name=f"grp{which}_{col0}_{a}", tag="grouped", bufs=3, align_bytes=64)
+            dst = grouped[:].rearrange("p (c i) t -> p c t i", i=4)
+            src = raw[(which, col0, a)][:].rearrange("p t (c i) -> p c t i", i=4)
+            if on_vector:
+                nc.vector.tensor_copy(out=dst, in_=src)
+            else:
+                nc.scalar.copy(out=dst, in_=src)
+            scales = keep.tile([P, width], U8, name=f"scales{which}_{col0}_{a}", align_bytes=64)
+            nc.vector.quantize_mx(out=codes.bitcast(FP8X4), scales=scales[:], in_=grouped[:].rearrange("p c t -> p (c t)"))
+            for c0 in range(0, width, P):
+                quant[(which, (col0 + c0) // P, a)] = (codes[:, c0 : c0 + P], scales[:, c0 : c0 + P])
+
+        def load_rows(dst, src, c):
+            nc.sync.dma_start(out=dst[:], in_=src[c * P : (c + 1) * P, :])
+
+        nc.vector.memset(tabs[:].bitcast(I32), 0)
+        for q in range(4):
+            nc.scalar.dma_start(
+                out=tabs[32 * q : 32 * q + 4, :, :].bitcast(I32),
+                in_=tab_scales[:, 4 * q : 4 * q + 4, :].rearrange("a r t -> r a t").bitcast(I32),
+            )
+        for q in range(4):
+            nc.gpsimd.dma_start(
+                out=w4s[32 * q : 32 * q + 4, :, :].bitcast(I32),
+                in_=w4_scales[:, 4 * q : 4 * q + 4, :].rearrange("a r t -> r a t").bitcast(I32),
+            )
+        make_identity(nc, ident_b[:])
+        make_identity(nc, ident_f[:])
+
+        nc.sync.dma_start(idx[:], offs)
+        nc.sync.dma_start(idx2[:], offs2)
+        nc.sync.dma_start(idx3[:], offs3)
+        with nc.allow_non_contiguous_dma(reason="one value a partition"):
+            nc.sync.dma_start(out=gain_t[:], in_=gain.rearrange("(c p) -> p c", p=P))
+        nc.sync.dma_start(out=tabw[0][:], in_=tab_words[0].rearrange("p t i -> p (t i)").bitcast(I32))
+        load_weight(1, w1, 0, P, 0)
+        load_weight(1, w1, 0, P, 1)
+        nc.sync.dma_start(out=tabw[1][:], in_=tab_words[1].rearrange("p t i -> p (t i)").bitcast(I32))
+        load_rows(site_t[0], site, 0)
+        nc.sync.dma_start(out=w4w[:].bitcast(I32), in_=w4_words.rearrange("a p n -> p a n").bitcast(I32))
+        load_weight(1, w1, P, P, 0)
+        load_weight(1, w1, P, P, 1)
+        nc.sync.dma_start(out=wgs_t[:], in_=wgs)
+        load_rows(page[0], page0, 0)
+        pairs = [(1, w1, c0) for c0 in range(2 * P, H, 2 * P)] + [(3, w3, c0) for c0 in range(0, H, 2 * P)]
+        for c in range(1, TILES):
+            which, w, c0 = pairs[c - 1]
+            for a in range(PASSES):
+                load_weight(which, w, c0, 2 * P, a)
+            if c > 1:
+                load_rows(page[c - 1], page0, c - 1)
+            load_rows(site_t[c], site, c)
+        load_rows(page[TILES - 1], page0, TILES - 1)
+        with nc.allow_non_contiguous_dma(reason="one value a partition"):
+            nc.sync.dma_start(out=stack_t[:], in_=stack.rearrange("(c p) -> p c", p=P))
+        for c in range(TILES):
+            load_rows(lim[c], limit, c)
+        nc.sync.dma_start(idx4[:], offs4)
+
+        nc.vector.tensor_copy(out=vw[0][:], in_=tabw[0][:].bitcast(U32).indirect(idx[:]))
+        for a in range(PASSES):
+            nc.vector.tensor_copy(out=vs[a][:], in_=tabs[:, a, :].indirect(idx[:]))
+        quantize_weight(1, 0, P, "first")
+        nc.vector.tensor_copy(out=vw[1][:], in_=tabw[1][:].bitcast(U32).indirect(idx[:]))
+
+        found = {}
+        p4 = {}
+        picked = {}
+        xt = [keep.tile([P, PICK // P, 2, P], F32, name=f"xt{a}") for a in range(PASSES)]
+        xq = {}
+
+        def products(c):
+            p1 = psum.tile([P, S], F32, name=f"p1_{c}", tag="p1", bufs=2)
+            p4[c] = psum.tile([P, S], F32, name=f"p4_{c}", tag="p4", bufs=1)
+            for a in range(PASSES):
+                codes, scales = quant[(1, c, a)]
+                nc.tensor.matmul_mx(
+                    out=p1[:], lhsT=codes.bitcast(FP8X4), lhsT_scale=scales,
+                    rhs=vw[a][:].bitcast(FP8X4), rhs_scale=vs[a][:], start=(a == 0), stop=(a == PASSES - 1),
+                )
+            for a in range(PASSES):
+                nc.tensor.matmul_mx(
+                    out=p4[c][:], lhsT=w4w[:, a, 2 * P * c : 2 * P * (c + 1)].bitcast(FP4X4),
+                    lhsT_scale=w4s[:, a, P * c : P * (c + 1)],
+                    rhs=vw[a][:].bitcast(FP8X4), rhs_scale=vs[a][:], start=(a == 0), stop=(a == PASSES - 1),
+                )
+            f = keep.tile([P, S], F32, name=f"f{c}", tag=f"f{c}", align_bytes=64)
+            nc.vector.tensor_tensor(out=f[:], in0=p1[:], in1=site_t[c][:], op=ALU.add)
+            found[c] = work.tile([P, S], F32, name=f"g{c}", tag="g", bufs=2)
+            nc.scalar.activation(out=found[c][:], in_=f[:], func=ACT.Gelu_apprx_tanh)
+
+        def add_second(c, h):
+            nc.vector.tensor_tensor(out=h[:], in0=p4[c][:], in1=found[c][:], op=ALU.add)
+
+        def put(c, h):
+            nc.vector.tensor_tensor(page[c][:].indirect(idx2[:]), h[:], wgs_t[:], ALU.mult)
+
+        def pick(c, dst):
+            nc.vector.tensor_copy(out=dst[:], in_=page[c][:].indirect(idx3[:]))
+            th = work.tile([P, PICK], F32, name=f"th{c}", tag="th", bufs=2)
+            nc.scalar.activation(out=th[:], in_=dst[:], func=ACT.Tanh)
+            xb = work.tile([P, PICK], BF16, name=f"xb{c}", tag="xb", bufs=2)
+            nc.scalar.activation(out=xb[:], in_=th[:], func=ACT.Copy, scale=gain_t[:, c : c + 1])
+            turned = psum.tile([P, PICK // P, P], BF16, name=f"turned{c}", tag="turned", bufs=1)
+            for b in range(PICK // P):
+                nc.tensor.transpose(turned[:, b, :], xb[:, b * P : (b + 1) * P], ident_b[:])
+            a, part = divmod(c, TILES_PER_PASS)
+            words = turned[:].rearrange("p b r -> p (b r)").bitcast(F32).rearrange("p (b q u) -> p b u q", b=PICK // P, u=2)
+            nc.scalar.copy(out=xt[a][:, :, :, 32 * part : 32 * (part + 1)], in_=words)
+
+        def quantize_x(a, tag, codes_tag):
+            xg = keep.tile([P, PICK, 2], F32, name=f"xg{a}", tag=tag, align_bytes=64)
+            codes = keep.tile([P, PICK], U32, name=f"xcodes{a}", tag=codes_tag, align_bytes=64)
+            scales = keep.tile([P, PICK], U8, name=f"xscales{a}", align_bytes=64)
+            for half in range(2):
+                back = psum.tile([P, 2, 2, P], F32, name=f"back{a}_{half}", tag="back", bufs=2)
+                for bb in range(2):
+                    for u in range(2):
+                        nc.tensor.transpose(back[:, bb, u, :], xt[a][:, 2 * half + bb, u, :], ident_f[:])
+                cols = slice(2 * P * half, 2 * P * (half + 1))
+                nc.scalar.copy(
+                    out=xg[:, cols, :].rearrange("p (b j) u -> p b j u", b=2),
+                    in_=back[:].rearrange("p b u j -> p b j u"),
+                )
+                nc.vector.quantize_mx(
+                    out=codes[:, cols].bitcast(FP8X4), scales=scales[:, cols],
+                    in_=xg[:, cols, :].rearrange("p j u -> p (j u)").bitcast(BF16),
+                )
+            xq[a] = (codes, scales)
+
+        products(0)
+        quantize_weight(1, P, P, "second")
+        for c in range(TILES):
+            h = work.tile([P, S], F32, name=f"h{c}", tag="h", bufs=2)
+            add_second(c, h)
+            if c > 0:
+                which, w, c0 = pairs[c - 1]
+                quantize_weight(which, c0, 2 * P, f"f{c}")
+            put(c, h)
+            if c + 1 < TILES:
+                products(c + 1)
+            if c == TILES - 1:
+                quantize_x(0, "xg0", "late")
+            if c + 1 < TILES and (c == 0):
+                pick(c, site_t[c + 1])
+            elif c == 5:
+                pick(c, keep.tile([P, PICK], F32, name=f"picked{c}", tag="late", align_bytes=64))
+            else:
+                pick(c, work.tile([P, PICK], F32, name=f"picked{c}", tag="picked", bufs=2))
+
+        shared = []
+        for n in range(TILES):
+            g4 = work.tile([P, PICK], F32, name=f"shared{n}", tag="shared", bufs=TILES)
+            nc.vector.tensor_copy(out=g4[:], in_=page[n][:].indirect(idx4[:]))
+            shared.append(g4)
+        quantize_x(1, "page2", "xcodes1")
+
+        banks = [("y", 2), ("y", 2), ("p1", 2), ("p1", 2), ("p4", 1), ("turned", 1), ("back", 2), ("back", 2)]
+        for n in range(TILES):
+            tag, bufs = banks[n]
+            y = psum.tile([P, PICK], F32, name=f"y{n}", tag=tag, bufs=bufs)
+            for a in range(PASSES):
+                codes, scales = quant[(3, n, a)]
+                nc.tensor.matmul_mx(
+                    out=y[:], lhsT=codes.bitcast(FP8X4), lhsT_scale=scales,
+                    rhs=xq[a][0][:].bitcast(FP8X4), rhs_scale=xq[a][1][:], start=(a == 0), stop=(a == PASSES - 1),
+                )
+            upper = work.tile([P, PICK], F32, name=f"upper{n}", tag="upper", bufs=4)
+            lower = work.tile([P, PICK], F32, name=f"lower{n}", tag="lower", bufs=4)
+            nc.vector.scalar_tensor_tensor(
+                out=upper[:], in0=shared[n][:], scalar=stack_t[:, n : n + 1], in1=y[:], op0=ALU.mult, op1=ALU.max
+            )
+            nc.vector.tensor_tensor(out=lower[:], in0=y[:], in1=lim[n][:], op=ALU.min)
+            res = work.tile([P, PICK], F32, name=f"res{n}", tag="res", bufs=3)
+            if n + 2 < TILES:
+                nc.gpsimd.tensor_tensor(out=res[:], in0=upper[:], in1=lower[:], op=ALU.add)
+            else:
+                nc.vector.tensor_tensor(out=res[:], in0=upper[:], in1=lower[:], op=ALU.add)
+            nc.sync.dma_start(out=out[n * P : (n + 1) * P, :], in_=res[:])

@@ -45,14 +45,16 @@ def tile_list_flue_register_review_kernel(
         tabs = keep.tile([P, PASSES, T], U8, name="tabs")
         vw = [keep.tile([P, S], U32, name=f"vw{a}", align_bytes=64) for a in range(PASSES)]
         vs = [keep.tile([P, S], U8, name=f"vs{a}", align_bytes=64) for a in range(PASSES)]
-        w4w = keep.tile([P, PASSES, 2 * H], U8, name="w4w", align_bytes=64)
+        early = 2 * 2 * P
+        w4_early = keep.tile([P, PASSES, early], U8, name="w4_early", align_bytes=64)
+        w4_rest = keep.tile([P, PASSES, 2 * H - early], U8, name="w4_rest", align_bytes=64)
         w4s = keep.tile([P, PASSES, H], U8, name="w4s", align_bytes=64)
         site_t = [keep.tile([P, S], F32, name=f"site{c}", tag=f"site{c}", align_bytes=64) for c in range(TILES)]
         page = [keep.tile([P, T2], F32, name=f"page{c}", tag=f"page{c}", align_bytes=64) for c in range(TILES)]
         lim = [keep.tile([P, PICK], F32, name=f"lim{c}") for c in range(TILES)]
         wgs_t = keep.tile([P, S], F32, name="wgs_t")
-        gain_t = keep.tile([P, TILES], F32, name="gain_t")
-        stack_t = keep.tile([P, TILES], F32, name="stack_t")
+        vec_rows = keep.tile([P, P], F32, name="vec_rows")
+        vec_cols = keep.tile([P, 2 * TILES], F32, name="vec_cols")
         ident_b = keep.tile([P, P], BF16, name="ident_b")
         ident_f = keep.tile([P, P], F32, name="ident_f")
 
@@ -60,24 +62,25 @@ def tile_list_flue_register_review_kernel(
         quant = {}
 
         def load_weight(which, w, col0, width, a):
-            t = work.tile([P, PACK, width], F32, name=f"raw{which}_{col0}_{a}", tag="raw", bufs=8)
+            t = work.tile([P, PACK, width], F32, name=f"raw{which}_{col0}_{a}", tag="raw", bufs=10)
             rows = w[a * PASS_K : (a + 1) * PASS_K, col0 : col0 + width]
             nc.sync.dma_start(out=t[:], in_=rows.rearrange("(p t) c -> p t c", t=PACK))
             raw[(which, col0, a)] = t
 
-        def quantize_weight(which, col0, width, tag, on_vector=False):
-            codes = keep.tile([P, PASSES, width], U32, name=f"codes{which}_{col0}", tag=tag, align_bytes=64)
-            for a in range(PASSES):
-                quantize_pass(which, col0, width, a, codes[:, a, :], on_vector)
+        def quantize_weights(pieces, tag):
+            total = PASSES * sum(width for which, w, col0, width in pieces)
+            codes = keep.tile([P, total], U32, name=f"codes_{tag}", tag=tag, align_bytes=64)
+            at = 0
+            for which, w, col0, width in pieces:
+                for a in range(PASSES):
+                    quantize_pass(which, col0, width, a, codes[:, at : at + width])
+                    at = at + width
 
-        def quantize_pass(which, col0, width, a, codes, on_vector):
-            grouped = work.tile([P, width, PACK], BF16, name=f"grp{which}_{col0}_{a}", tag="grouped", bufs=3, align_bytes=64)
+        def quantize_pass(which, col0, width, a, codes):
+            grouped = work.tile([P, width, PACK], BF16, name=f"grp{which}_{col0}_{a}", tag="grouped", bufs=6, align_bytes=64)
             dst = grouped[:].rearrange("p (c i) t -> p c t i", i=4)
             src = raw[(which, col0, a)][:].rearrange("p t (c i) -> p c t i", i=4)
-            if on_vector:
-                nc.vector.tensor_copy(out=dst, in_=src)
-            else:
-                nc.scalar.copy(out=dst, in_=src)
+            nc.scalar.copy(out=dst, in_=src)
             scales = keep.tile([P, width], U8, name=f"scales{which}_{col0}_{a}", align_bytes=64)
             nc.vector.quantize_mx(out=codes.bitcast(FP8X4), scales=scales[:], in_=grouped[:].rearrange("p c t -> p (c t)"))
             for c0 in range(0, width, P):
@@ -97,35 +100,45 @@ def tile_list_flue_register_review_kernel(
                 out=w4s[32 * q : 32 * q + 4, :, :].bitcast(I32),
                 in_=w4_scales[:, 4 * q : 4 * q + 4, :].rearrange("a r t -> r a t").bitcast(I32),
             )
-        make_identity(nc, ident_b[:])
+        nc.gpsimd.memset(vec_rows[:], 0.0)
+        nc.gpsimd.dma_start(out=vec_rows[0:TILES, :], in_=gain.rearrange("(c p) -> c p", p=P))
+        nc.gpsimd.dma_start(out=vec_rows[TILES : 2 * TILES, :], in_=stack.rearrange("(c p) -> c p", p=P))
         make_identity(nc, ident_f[:])
+        make_identity(nc, ident_b[:])
 
         nc.sync.dma_start(idx[:], offs)
         nc.sync.dma_start(idx2[:], offs2)
         nc.sync.dma_start(idx3[:], offs3)
-        with nc.allow_non_contiguous_dma(reason="one value a partition"):
-            nc.sync.dma_start(out=gain_t[:], in_=gain.rearrange("(c p) -> p c", p=P))
-        nc.sync.dma_start(out=tabw[0][:], in_=tab_words[0].rearrange("p t i -> p (t i)").bitcast(I32))
+        w4_view = w4_words.rearrange("a p n -> p a n")
         load_weight(1, w1, 0, P, 0)
+        nc.sync.dma_start(out=tabw[0][:], in_=tab_words[0].rearrange("p t i -> p (t i)").bitcast(I32))
         load_weight(1, w1, 0, P, 1)
         nc.sync.dma_start(out=tabw[1][:], in_=tab_words[1].rearrange("p t i -> p (t i)").bitcast(I32))
+        nc.sync.dma_start(out=w4_early[:].bitcast(I32), in_=w4_view[:, :, :early].bitcast(I32))
         load_rows(site_t[0], site, 0)
-        nc.sync.dma_start(out=w4w[:].bitcast(I32), in_=w4_words.rearrange("a p n -> p a n").bitcast(I32))
         load_weight(1, w1, P, P, 0)
         load_weight(1, w1, P, P, 1)
         nc.sync.dma_start(out=wgs_t[:], in_=wgs)
         load_rows(page[0], page0, 0)
-        pairs = [(1, w1, c0) for c0 in range(2 * P, H, 2 * P)] + [(3, w3, c0) for c0 in range(0, H, 2 * P)]
+        pieces_of = {
+            1: [(1, w1, 2 * P, P)],
+            2: [(1, w1, 3 * P, 2 * P)],
+            3: [(1, w1, 5 * P, 2 * P)],
+            4: [(1, w1, 7 * P, P), (3, w3, 0, P)],
+            5: [(3, w3, P, 2 * P)],
+            6: [(3, w3, 3 * P, 2 * P)],
+            7: [(3, w3, 5 * P, 2 * P), (3, w3, 7 * P, P)],
+        }
         for c in range(1, TILES):
-            which, w, c0 = pairs[c - 1]
-            for a in range(PASSES):
-                load_weight(which, w, c0, 2 * P, a)
+            for which, w, c0, width in pieces_of[c]:
+                for a in range(PASSES):
+                    load_weight(which, w, c0, width, a)
+            if c == 2:
+                nc.sync.dma_start(out=w4_rest[:].bitcast(I32), in_=w4_view[:, :, early:].bitcast(I32))
             if c > 1:
                 load_rows(page[c - 1], page0, c - 1)
             load_rows(site_t[c], site, c)
         load_rows(page[TILES - 1], page0, TILES - 1)
-        with nc.allow_non_contiguous_dma(reason="one value a partition"):
-            nc.sync.dma_start(out=stack_t[:], in_=stack.rearrange("(c p) -> p c", p=P))
         for c in range(TILES):
             load_rows(lim[c], limit, c)
         nc.sync.dma_start(idx4[:], offs4)
@@ -133,7 +146,7 @@ def tile_list_flue_register_review_kernel(
         nc.vector.tensor_copy(out=vw[0][:], in_=tabw[0][:].bitcast(U32).indirect(idx[:]))
         for a in range(PASSES):
             nc.vector.tensor_copy(out=vs[a][:], in_=tabs[:, a, :].indirect(idx[:]))
-        quantize_weight(1, 0, P, "first")
+        quantize_weights([(1, w1, 0, P)], "first")
         nc.vector.tensor_copy(out=vw[1][:], in_=tabw[1][:].bitcast(U32).indirect(idx[:]))
 
         found = {}
@@ -151,9 +164,10 @@ def tile_list_flue_register_review_kernel(
                     out=p1[:], lhsT=codes.bitcast(FP8X4), lhsT_scale=scales,
                     rhs=vw[a][:].bitcast(FP8X4), rhs_scale=vs[a][:], start=(a == 0), stop=(a == PASSES - 1),
                 )
+            w4w, byte0 = (w4_early, 2 * P * c) if 2 * P * c < early else (w4_rest, 2 * P * c - early)
             for a in range(PASSES):
                 nc.tensor.matmul_mx(
-                    out=p4[c][:], lhsT=w4w[:, a, 2 * P * c : 2 * P * (c + 1)].bitcast(FP4X4),
+                    out=p4[c][:], lhsT=w4w[:, a, byte0 : byte0 + 2 * P].bitcast(FP4X4),
                     lhsT_scale=w4s[:, a, P * c : P * (c + 1)],
                     rhs=vw[a][:].bitcast(FP8X4), rhs_scale=vs[a][:], start=(a == 0), stop=(a == PASSES - 1),
                 )
@@ -173,7 +187,7 @@ def tile_list_flue_register_review_kernel(
             th = work.tile([P, PICK], F32, name=f"th{c}", tag="th", bufs=2)
             nc.scalar.activation(out=th[:], in_=dst[:], func=ACT.Tanh)
             xb = work.tile([P, PICK], BF16, name=f"xb{c}", tag="xb", bufs=2)
-            nc.scalar.activation(out=xb[:], in_=th[:], func=ACT.Copy, scale=gain_t[:, c : c + 1])
+            nc.scalar.activation(out=xb[:], in_=th[:], func=ACT.Copy, scale=vec_cols[:, c : c + 1])
             turned = psum.tile([P, PICK // P, P], BF16, name=f"turned{c}", tag="turned", bufs=1)
             for b in range(PICK // P):
                 nc.tensor.transpose(turned[:, b, :], xb[:, b * P : (b + 1) * P], ident_b[:])
@@ -202,28 +216,30 @@ def tile_list_flue_register_review_kernel(
             xq[a] = (codes, scales)
 
         products(0)
-        quantize_weight(1, P, P, "second")
+        quantize_weights([(1, w1, P, P)], "second")
+        vec_turned = psum.tile([P, P], F32, name="vec_turned", tag="back", bufs=2)
+        nc.tensor.transpose(vec_turned[:], vec_rows[:], ident_f[:])
+        nc.scalar.copy(out=vec_cols[:], in_=vec_turned[:, : 2 * TILES])
         for c in range(TILES):
             h = work.tile([P, S], F32, name=f"h{c}", tag="h", bufs=2)
             add_second(c, h)
             if c > 0:
-                which, w, c0 = pairs[c - 1]
-                quantize_weight(which, c0, 2 * P, f"f{c}")
+                quantize_weights(pieces_of[c], f"f{c}")
             put(c, h)
             if c + 1 < TILES:
                 products(c + 1)
             if c == TILES - 1:
-                quantize_x(0, "xg0", "late")
+                quantize_x(0, "xg0", "late5")
             if c + 1 < TILES and (c == 0):
                 pick(c, site_t[c + 1])
             elif c == 5:
-                pick(c, keep.tile([P, PICK], F32, name=f"picked{c}", tag="late", align_bytes=64))
+                pick(c, keep.tile([P, PICK], F32, name=f"picked{c}", tag=f"late{c}", align_bytes=64))
             else:
                 pick(c, work.tile([P, PICK], F32, name=f"picked{c}", tag="picked", bufs=2))
 
         shared = []
         for n in range(TILES):
-            g4 = work.tile([P, PICK], F32, name=f"shared{n}", tag="shared", bufs=TILES)
+            g4 = keep.tile([P, PICK], F32, name=f"shared{n}", tag=f"site{n}", align_bytes=64)
             nc.vector.tensor_copy(out=g4[:], in_=page[n][:].indirect(idx4[:]))
             shared.append(g4)
         quantize_x(1, "page2", "xcodes1")
@@ -241,7 +257,7 @@ def tile_list_flue_register_review_kernel(
             upper = work.tile([P, PICK], F32, name=f"upper{n}", tag="upper", bufs=4)
             lower = work.tile([P, PICK], F32, name=f"lower{n}", tag="lower", bufs=4)
             nc.vector.scalar_tensor_tensor(
-                out=upper[:], in0=shared[n][:], scalar=stack_t[:, n : n + 1], in1=y[:], op0=ALU.mult, op1=ALU.max
+                out=upper[:], in0=shared[n][:], scalar=vec_cols[:, TILES + n : TILES + n + 1], in1=y[:], op0=ALU.mult, op1=ALU.max
             )
             nc.vector.tensor_tensor(out=lower[:], in0=y[:], in1=lim[n][:], op=ALU.min)
             res = work.tile([P, PICK], F32, name=f"res{n}", tag="res", bufs=3)

@@ -54,7 +54,6 @@ def tile_list_flue_register_review_kernel(
         lim = [keep.tile([P, PICK], F32, name=f"lim{c}") for c in range(TILES)]
         wgs_t = keep.tile([P, S], F32, name="wgs_t")
         vec_rows = keep.tile([P, P], F32, name="vec_rows")
-        vec_cols = keep.tile([P, 2 * TILES], F32, name="vec_cols")
         ident_b = keep.tile([P, P], BF16, name="ident_b")
         ident_f = keep.tile([P, P], F32, name="ident_f")
 
@@ -67,20 +66,20 @@ def tile_list_flue_register_review_kernel(
             nc.sync.dma_start(out=t[:], in_=rows.rearrange("(p t) c -> p t c", t=PACK))
             raw[(which, col0, a)] = t
 
-        def quantize_weights(pieces, tag):
+        def quantize_weights(pieces, tag, interleave):
             total = PASSES * sum(width for which, w, col0, width in pieces)
             codes = keep.tile([P, total], U32, name=f"codes_{tag}", tag=tag, align_bytes=64)
             at = 0
             for which, w, col0, width in pieces:
                 for a in range(PASSES):
-                    quantize_pass(which, col0, width, a, codes[:, at : at + width])
+                    quantize_pass(which, col0, width, a, codes[:, at : at + width], interleave)
                     at = at + width
 
-        def quantize_pass(which, col0, width, a, codes):
+        def quantize_pass(which, col0, width, a, codes, interleave):
             grouped = work.tile([P, width, PACK], BF16, name=f"grp{which}_{col0}_{a}", tag="grouped", bufs=6, align_bytes=64)
             dst = grouped[:].rearrange("p (c i) t -> p c t i", i=4)
             src = raw[(which, col0, a)][:].rearrange("p t (c i) -> p c t i", i=4)
-            nc.scalar.copy(out=dst, in_=src)
+            interleave(out=dst, in_=src)
             scales = keep.tile([P, width], U8, name=f"scales{which}_{col0}_{a}", align_bytes=64)
             nc.vector.quantize_mx(out=codes.bitcast(FP8X4), scales=scales[:], in_=grouped[:].rearrange("p c t -> p (c t)"))
             for c0 in range(0, width, P):
@@ -120,24 +119,18 @@ def tile_list_flue_register_review_kernel(
         load_weight(1, w1, P, P, 1)
         nc.sync.dma_start(out=wgs_t[:], in_=wgs)
         load_rows(page[0], page0, 0)
-        pieces_of = {
-            1: [(1, w1, 2 * P, P)],
-            2: [(1, w1, 3 * P, 2 * P)],
-            3: [(1, w1, 5 * P, 2 * P)],
-            4: [(1, w1, 7 * P, P), (3, w3, 0, P)],
-            5: [(3, w3, P, 2 * P)],
-            6: [(3, w3, 3 * P, 2 * P)],
-            7: [(3, w3, 5 * P, 2 * P), (3, w3, 7 * P, P)],
-        }
+        pairs = [(1, w1, c0, 2 * P) for c0 in range(2 * P, H, 2 * P)] + [(3, w3, c0, 2 * P) for c0 in range(0, H, 2 * P)]
+        sites_after = {1: [1], 2: [2, 3], 3: [4], 4: [5], 5: [6], 6: [7], 7: []}
         for c in range(1, TILES):
-            for which, w, c0, width in pieces_of[c]:
-                for a in range(PASSES):
-                    load_weight(which, w, c0, width, a)
+            which, w, c0, width = pairs[c - 1]
+            for a in range(PASSES):
+                load_weight(which, w, c0, width, a)
             if c == 2:
                 nc.sync.dma_start(out=w4_rest[:].bitcast(I32), in_=w4_view[:, :, early:].bitcast(I32))
             if c > 1:
                 load_rows(page[c - 1], page0, c - 1)
-            load_rows(site_t[c], site, c)
+            for j in sites_after[c]:
+                load_rows(site_t[j], site, j)
         load_rows(page[TILES - 1], page0, TILES - 1)
         for c in range(TILES):
             load_rows(lim[c], limit, c)
@@ -146,7 +139,7 @@ def tile_list_flue_register_review_kernel(
         nc.vector.tensor_copy(out=vw[0][:], in_=tabw[0][:].bitcast(U32).indirect(idx[:]))
         for a in range(PASSES):
             nc.vector.tensor_copy(out=vs[a][:], in_=tabs[:, a, :].indirect(idx[:]))
-        quantize_weights([(1, w1, 0, P)], "first")
+        quantize_weights([(1, w1, 0, P)], "first", nc.scalar.copy)
         nc.vector.tensor_copy(out=vw[1][:], in_=tabw[1][:].bitcast(U32).indirect(idx[:]))
 
         found = {}
@@ -173,11 +166,16 @@ def tile_list_flue_register_review_kernel(
                 )
             f = keep.tile([P, S], F32, name=f"f{c}", tag=f"f{c}", align_bytes=64)
             nc.vector.tensor_tensor(out=f[:], in0=p1[:], in1=site_t[c][:], op=ALU.add)
-            found[c] = work.tile([P, S], F32, name=f"g{c}", tag="g", bufs=2)
+            found[c] = work.tile([P, S], F32, name=f"g{c}", tag="g", bufs=3)
             nc.scalar.activation(out=found[c][:], in_=f[:], func=ACT.Gelu_apprx_tanh)
 
         def add_second(c, h):
             nc.vector.tensor_tensor(out=h[:], in0=p4[c][:], in1=found[c][:], op=ALU.add)
+
+        def add_second_aside(c, h):
+            second = keep.tile([P, S], F32, name=f"second{c}", tag=f"site{c}", align_bytes=64)
+            nc.scalar.copy(out=second[:], in_=p4[c][:])
+            nc.gpsimd.tensor_tensor(out=h[:], in0=second[:], in1=found[c][:], op=ALU.add)
 
         def put(c, h):
             nc.vector.tensor_tensor(page[c][:].indirect(idx2[:]), h[:], wgs_t[:], ALU.mult)
@@ -216,30 +214,46 @@ def tile_list_flue_register_review_kernel(
             xq[a] = (codes, scales)
 
         products(0)
-        quantize_weights([(1, w1, P, P)], "second")
+        quantize_weights([(1, w1, P, P)], "second", nc.vector.tensor_copy)
         vec_turned = psum.tile([P, P], F32, name="vec_turned", tag="back", bufs=2)
         nc.tensor.transpose(vec_turned[:], vec_rows[:], ident_f[:])
+        vec_cols = keep.tile([P, 2 * TILES], F32, name="vec_cols", tag="f0", align_bytes=64)
         nc.scalar.copy(out=vec_cols[:], in_=vec_turned[:, : 2 * TILES])
-        for c in range(TILES):
-            h = work.tile([P, S], F32, name=f"h{c}", tag="h", bufs=2)
-            add_second(c, h)
-            if c > 0:
-                quantize_weights(pieces_of[c], f"f{c}")
-            put(c, h)
-            if c + 1 < TILES:
-                products(c + 1)
-            if c == TILES - 1:
-                quantize_x(0, "xg0", "late5")
-            if c + 1 < TILES and (c == 0):
-                pick(c, site_t[c + 1])
+        def pick_into(c):
+            if c == 0:
+                pick(c, site_t[1])
             elif c == 5:
-                pick(c, keep.tile([P, PICK], F32, name=f"picked{c}", tag=f"late{c}", align_bytes=64))
+                pick(c, keep.tile([P, PICK], F32, name=f"picked{c}", tag="late5", align_bytes=64))
             else:
                 pick(c, work.tile([P, PICK], F32, name=f"picked{c}", tag="picked", bufs=2))
 
+        ahead = 3
+        for c in range(TILES):
+            h = work.tile([P, S], F32, name=f"h{c}", tag="h", bufs=1)
+            if c < ahead:
+                if c > 0:
+                    products(c)
+                    pick_into(c - 1)
+                add_second(c, h)
+                if c == ahead - 1:
+                    products(c + 1)
+                tie = f"f{c}"
+            else:
+                add_second_aside(c, h)
+                if c + 1 < TILES:
+                    products(c + 1)
+                pick_into(c - 1)
+                tie = f"site{c}"
+            if c > 0:
+                quantize_weights([pairs[c - 1]], tie, nc.scalar.copy)
+            if c == TILES - 1:
+                quantize_x(0, "xg0", "late5")
+            put(c, h)
+        pick_into(TILES - 1)
+
         shared = []
         for n in range(TILES):
-            g4 = keep.tile([P, PICK], F32, name=f"shared{n}", tag=f"site{n}", align_bytes=64)
+            g4 = keep.tile([P, PICK], F32, name=f"shared{n}", tag=(f"site{n}" if n < ahead else f"f{n}"), align_bytes=64)
             nc.vector.tensor_copy(out=g4[:], in_=page[n][:].indirect(idx4[:]))
             shared.append(g4)
         quantize_x(1, "page2", "xcodes1")

@@ -125,12 +125,12 @@ def tile_list_flue_register_review_kernel(
             which, w, c0, width = pairs[c - 1]
             for a in range(PASSES):
                 load_weight(which, w, c0, width, a)
-            if c == 2:
-                nc.sync.dma_start(out=w4_rest[:].bitcast(I32), in_=w4_view[:, :, early:].bitcast(I32))
             if c > 1:
                 load_rows(page[c - 1], page0, c - 1)
             for j in sites_after[c]:
                 load_rows(site_t[j], site, j)
+            if c == 2:
+                nc.sync.dma_start(out=w4_rest[:].bitcast(I32), in_=w4_view[:, :, early:].bitcast(I32))
         load_rows(page[TILES - 1], page0, TILES - 1)
         for c in range(TILES):
             load_rows(lim[c], limit, c)
@@ -251,12 +251,16 @@ def tile_list_flue_register_review_kernel(
             put(c, h)
         pick_into(TILES - 1)
 
-        shared = []
-        for n in range(TILES):
-            g4 = keep.tile([P, PICK], F32, name=f"shared{n}", tag=(f"site{n}" if n < ahead else f"f{n}"), align_bytes=64)
-            nc.vector.tensor_copy(out=g4[:], in_=page[n][:].indirect(idx4[:]))
-            shared.append(g4)
+        shared = {}
+
+        def pick_shared(n, tag):
+            shared[n] = keep.tile([P, PICK], F32, name=f"shared{n}", tag=tag, align_bytes=64)
+            nc.vector.tensor_copy(out=shared[n][:], in_=page[n][:].indirect(idx4[:]))
+
+        for n in range(TILES - 2):
+            pick_shared(n, f"site{n}" if n < ahead else f"f{n}")
         quantize_x(1, "page2", "xcodes1")
+        pick_shared(TILES - 2, "page2")
 
         banks = [("y", 2), ("y", 2), ("p1", 2), ("p1", 2), ("p4", 1), ("turned", 1), ("back", 2), ("back", 2)]
         for n in range(TILES):
@@ -268,15 +272,22 @@ def tile_list_flue_register_review_kernel(
                     out=y[:], lhsT=codes.bitcast(FP8X4), lhsT_scale=scales,
                     rhs=xq[a][0][:].bitcast(FP8X4), rhs_scale=xq[a][1][:], start=(a == 0), stop=(a == PASSES - 1),
                 )
-            upper = work.tile([P, PICK], F32, name=f"upper{n}", tag="upper", bufs=4)
-            lower = work.tile([P, PICK], F32, name=f"lower{n}", tag="lower", bufs=4)
-            nc.vector.scalar_tensor_tensor(
-                out=upper[:], in0=shared[n][:], scalar=vec_cols[:, TILES + n : TILES + n + 1], in1=y[:], op0=ALU.mult, op1=ALU.max
-            )
-            nc.vector.tensor_tensor(out=lower[:], in0=y[:], in1=lim[n][:], op=ALU.min)
-            res = work.tile([P, PICK], F32, name=f"res{n}", tag="res", bufs=3)
-            if n + 2 < TILES:
-                nc.gpsimd.tensor_tensor(out=res[:], in0=upper[:], in1=lower[:], op=ALU.add)
-            else:
-                nc.vector.tensor_tensor(out=res[:], in0=upper[:], in1=lower[:], op=ALU.add)
-            nc.sync.dma_start(out=out[n * P : (n + 1) * P, :], in_=res[:])
+            if n == TILES - 1:
+                pick_shared(n, "f5")
+            parts = 2 if n == TILES - 1 else 1
+            width = PICK // parts
+            pending = []
+            for part in range(parts):
+                cols = slice(part * width, (part + 1) * width)
+                upper = work.tile([P, width], F32, name=f"upper{n}_{part}", tag="upper", bufs=4)
+                lower = work.tile([P, width], F32, name=f"lower{n}_{part}", tag="lower", bufs=4)
+                nc.vector.scalar_tensor_tensor(
+                    out=upper[:], in0=shared[n][:, cols], scalar=vec_cols[:, TILES + n : TILES + n + 1],
+                    in1=y[:, cols], op0=ALU.mult, op1=ALU.max,
+                )
+                nc.vector.tensor_tensor(out=lower[:], in0=y[:, cols], in1=lim[n][:, cols], op=ALU.min)
+                pending.append((cols, upper, lower))
+            for cols, upper, lower in pending:
+                adder = nc.gpsimd if n + 1 < TILES else nc.vector
+                adder.tensor_tensor(out=lim[n][:, cols], in0=upper[:], in1=lower[:], op=ALU.add)
+                nc.sync.dma_start(out=out[n * P : (n + 1) * P, cols], in_=lim[n][:, cols])

from contextlib import ExitStack

import concourse.mybir as mybir
from concourse.masks import make_identity

K, H, T, S, T2, PICK = 1024, 1024, 2048, 512, 1024, 512
FLOPS = 3 * 2 * 1024 * 1024 * 512

F32 = mybir.dt.float32
BF16 = mybir.dt.bfloat16
I32 = mybir.dt.int32
U32 = mybir.dt.uint32
U16 = mybir.dt.uint16
U8 = mybir.dt.uint8
FP8X4 = mybir.dt.float8_e4m3fn_x4
FP4X4 = mybir.dt.float4_e2m1fn_x4
ALU = mybir.AluOpType
ACT = mybir.ActivationFunctionType

P = 128
PACK = 4
PASS_K = P * PACK
PASSES = K // PASS_K
TILES = H // P
TILES_PER_PASS = PASS_K // P


def tile_list_flue_register_review_kernel(
    tc, tab_words, tab_scales, offs, w1, site, w4_words, w4_scales, page0, wgs,
    offs2, offs3, offs4, gain, w3, stack, limit, out,
):
    nc = tc.nc
    with ExitStack() as ctx:
        lists = ctx.enter_context(tc.tile_pool(name="lists", bufs=1))
        keep = ctx.enter_context(tc.tile_pool(name="keep", bufs=1))
        work = ctx.enter_context(tc.tile_pool(name="work", bufs=2))
        psum = ctx.enter_context(tc.psum_pool(name="psum", bufs=1))

        idx = lists.tile([P, S // 16], U16, name="idx")
        idx2 = lists.tile([P, S // 16], U16, name="idx2")
        idx3 = lists.tile([P, PICK // 16], U16, name="idx3")
        idx4 = lists.tile([P, PICK // 16], U16, name="idx4")

        tabw = [keep.tile([P, T], I32, name=f"tabw{a}") for a in range(PASSES)]
        tabs = keep.tile([P, PASSES, T], U8, name="tabs")
        vw = [keep.tile([P, S], U32, name=f"vw{a}", align_bytes=64) for a in range(PASSES)]
        vs = [keep.tile([P, S], U8, name=f"vs{a}", align_bytes=64) for a in range(PASSES)]
        early = 2 * 2 * P
        w4_early = keep.tile([P, PASSES, early], U8, name="w4_early", align_bytes=64)
        w4_rest = keep.tile([P, PASSES, 2 * H - early], U8, name="w4_rest", align_bytes=64)
        w4s = keep.tile([P, PASSES, H], U8, name="w4s", align_bytes=64)
        site_t = [keep.tile([P, S], F32, name=f"site{c}", tag=f"site{c}", align_bytes=64) for c in range(TILES)]
        page = [keep.tile([P, T2], F32, name=f"page{c}", tag=f"page{c}", align_bytes=64) for c in range(TILES)]
        lim = [keep.tile([P, PICK], F32, name=f"lim{c}") for c in range(TILES)]
        wgs_t = keep.tile([P, S], F32, name="wgs_t")
        vec_rows = keep.tile([P, P], F32, name="vec_rows")
        ident_b = keep.tile([P, P], BF16, name="ident_b")
        ident_f = keep.tile([P, P], F32, name="ident_f")

        raw = {}
        quant = {}

        def load_weight(which, w, col0, width, a):
            t = work.tile([P, PACK, width], F32, name=f"raw{which}_{col0}_{a}", tag="raw", bufs=10)
            rows = w[a * PASS_K : (a + 1) * PASS_K, col0 : col0 + width]
            nc.sync.dma_start(out=t[:], in_=rows.rearrange("(p t) c -> p t c", t=PACK))
            raw[(which, col0, a)] = t

        def quantize_weights(pieces, tag, interleave):
            total = PASSES * sum(width for which, w, col0, width in pieces)
            codes = keep.tile([P, total], U32, name=f"codes_{tag}", tag=tag, align_bytes=64)
            at = 0
            for which, w, col0, width in pieces:
                for a in range(PASSES):
                    quantize_pass(which, col0, width, a, codes[:, at : at + width], interleave)
                    at = at + width

        def quantize_pass(which, col0, width, a, codes, interleave):
            grouped = work.tile([P, width, PACK], BF16, name=f"grp{which}_{col0}_{a}", tag="grouped", bufs=6, align_bytes=64)
            dst = grouped[:].rearrange("p (c i) t -> p c t i", i=4)
            src = raw[(which, col0, a)][:].rearrange("p t (c i) -> p c t i", i=4)
            interleave(out=dst, in_=src)
            scales = keep.tile([P, width], U8, name=f"scales{which}_{col0}_{a}", align_bytes=64)
            nc.vector.quantize_mx(out=codes.bitcast(FP8X4), scales=scales[:], in_=grouped[:].rearrange("p c t -> p (c t)"))
            for c0 in range(0, width, P):
                quant[(which, (col0 + c0) // P, a)] = (codes[:, c0 : c0 + P], scales[:, c0 : c0 + P])

        def load_rows(dst, src, c):
            nc.sync.dma_start(out=dst[:], in_=src[c * P : (c + 1) * P, :])

        nc.vector.memset(tabs[:].bitcast(I32), 0)
        for q in range(4):
            nc.scalar.dma_start(
                out=tabs[32 * q : 32 * q + 4, :, :].bitcast(I32),
                in_=tab_scales[:, 4 * q : 4 * q + 4, :].rearrange("a r t -> r a t").bitcast(I32),
            )
        for q in range(4):
            nc.gpsimd.dma_start(
                out=w4s[32 * q : 32 * q + 4, :, :].bitcast(I32),
                in_=w4_scales[:, 4 * q : 4 * q + 4, :].rearrange("a r t -> r a t").bitcast(I32),
            )
        nc.gpsimd.memset(vec_rows[:], 0.0)
        nc.gpsimd.dma_start(out=vec_rows[0:TILES, :], in_=gain.rearrange("(c p) -> c p", p=P))
        nc.gpsimd.dma_start(out=vec_rows[TILES : 2 * TILES, :], in_=stack.rearrange("(c p) -> c p", p=P))
        make_identity(nc, ident_f[:])
        make_identity(nc, ident_b[:])

        nc.sync.dma_start(idx[:], offs)
        nc.sync.dma_start(idx2[:], offs2)
        nc.sync.dma_start(idx3[:], offs3)
        w4_view = w4_words.rearrange("a p n -> p a n")
        load_weight(1, w1, 0, P, 0)
        nc.sync.dma_start(out=tabw[0][:], in_=tab_words[0].rearrange("p t i -> p (t i)").bitcast(I32))
        load_weight(1, w1, 0, P, 1)
        nc.sync.dma_start(out=tabw[1][:], in_=tab_words[1].rearrange("p t i -> p (t i)").bitcast(I32))
        nc.sync.dma_start(out=w4_early[:].bitcast(I32), in_=w4_view[:, :, :early].bitcast(I32))
        load_rows(site_t[0], site, 0)
        load_weight(1, w1, P, P, 0)
        load_weight(1, w1, P, P, 1)
        nc.sync.dma_start(out=wgs_t[:], in_=wgs)
        load_rows(page[0], page0, 0)
        pairs = [(1, w1, c0, 2 * P) for c0 in range(2 * P, H, 2 * P)] + [(3, w3, c0, 2 * P) for c0 in range(0, H, 2 * P)]
        sites_after = {1: [1], 2: [2, 3], 3: [4], 4: [5], 5: [6], 6: [7], 7: []}
        for c in range(1, TILES):
            which, w, c0, width = pairs[c - 1]
            for a in range(PASSES):
                load_weight(which, w, c0, width, a)
            if c > 1:
                load_rows(page[c - 1], page0, c - 1)
            for j in sites_after[c]:
                load_rows(site_t[j], site, j)
            if c == 2:
                nc.sync.dma_start(out=w4_rest[:].bitcast(I32), in_=w4_view[:, :, early:].bitcast(I32))
        load_rows(page[TILES - 1], page0, TILES - 1)
        for c in range(TILES):
            load_rows(lim[c], limit, c)
        nc.sync.dma_start(idx4[:], offs4)

        nc.vector.tensor_copy(out=vw[0][:], in_=tabw[0][:].bitcast(U32).indirect(idx[:]))
        for a in range(PASSES):
            nc.vector.tensor_copy(out=vs[a][:], in_=tabs[:, a, :].indirect(idx[:]))
        quantize_weights([(1, w1, 0, P)], "first", nc.scalar.copy)
        nc.vector.tensor_copy(out=vw[1][:], in_=tabw[1][:].bitcast(U32).indirect(idx[:]))

        found = {}
        p4 = {}
        picked = {}
        xt = [keep.tile([P, PICK // P, 2, P], F32, name=f"xt{a}") for a in range(PASSES)]
        xq = {}

        def products(c):
            p1 = psum.tile([P, S], F32, name=f"p1_{c}", tag="p1", bufs=2)
            p4[c] = psum.tile([P, S], F32, name=f"p4_{c}", tag="p4", bufs=1)
            for a in range(PASSES):
                codes, scales = quant[(1, c, a)]
                nc.tensor.matmul_mx(
                    out=p1[:], lhsT=codes.bitcast(FP8X4), lhsT_scale=scales,
                    rhs=vw[a][:].bitcast(FP8X4), rhs_scale=vs[a][:], start=(a == 0), stop=(a == PASSES - 1),
                )
            w4w, byte0 = (w4_early, 2 * P * c) if 2 * P * c < early else (w4_rest, 2 * P * c - early)
            for a in range(PASSES):
                nc.tensor.matmul_mx(
                    out=p4[c][:], lhsT=w4w[:, a, byte0 : byte0 + 2 * P].bitcast(FP4X4),
                    lhsT_scale=w4s[:, a, P * c : P * (c + 1)],
                    rhs=vw[a][:].bitcast(FP8X4), rhs_scale=vs[a][:], start=(a == 0), stop=(a == PASSES - 1),
                )
            f = keep.tile([P, S], F32, name=f"f{c}", tag=f"f{c}", align_bytes=64)
            nc.vector.tensor_tensor(out=f[:], in0=p1[:], in1=site_t[c][:], op=ALU.add)
            found[c] = work.tile([P, S], F32, name=f"g{c}", tag="g", bufs=3)
            nc.scalar.activation(out=found[c][:], in_=f[:], func=ACT.Gelu_apprx_tanh)

        def add_second(c, h):
            nc.vector.tensor_tensor(out=h[:], in0=p4[c][:], in1=found[c][:], op=ALU.add)

        def add_second_aside(c, h):
            second = keep.tile([P, S], F32, name=f"second{c}", tag=f"site{c}", align_bytes=64)
            nc.scalar.copy(out=second[:], in_=p4[c][:])
            nc.gpsimd.tensor_tensor(out=h[:], in0=second[:], in1=found[c][:], op=ALU.add)

        def put(c, h):
            nc.vector.tensor_tensor(page[c][:].indirect(idx2[:]), h[:], wgs_t[:], ALU.mult)

        def pick(c, dst):
            nc.vector.tensor_copy(out=dst[:], in_=page[c][:].indirect(idx3[:]))
            th = work.tile([P, PICK], F32, name=f"th{c}", tag="th", bufs=2)
            nc.scalar.activation(out=th[:], in_=dst[:], func=ACT.Tanh)
            xb = work.tile([P, PICK], BF16, name=f"xb{c}", tag="xb", bufs=2)
            nc.scalar.activation(out=xb[:], in_=th[:], func=ACT.Copy, scale=vec_cols[:, c : c + 1])
            turned = psum.tile([P, PICK // P, P], BF16, name=f"turned{c}", tag="turned", bufs=1)
            for b in range(PICK // P):
                nc.tensor.transpose(turned[:, b, :], xb[:, b * P : (b + 1) * P], ident_b[:])
            a, part = divmod(c, TILES_PER_PASS)
            words = turned[:].rearrange("p b r -> p (b r)").bitcast(F32).rearrange("p (b q u) -> p b u q", b=PICK // P, u=2)
            nc.scalar.copy(out=xt[a][:, :, :, 32 * part : 32 * (part + 1)], in_=words)

        def quantize_x(a, tag, codes_tag):
            xg = keep.tile([P, PICK, 2], F32, name=f"xg{a}", tag=tag, align_bytes=64)
            codes = keep.tile([P, PICK], U32, name=f"xcodes{a}", tag=codes_tag, align_bytes=64)
            scales = keep.tile([P, PICK], U8, name=f"xscales{a}", align_bytes=64)
            for half in range(2):
                back = psum.tile([P, 2, 2, P], F32, name=f"back{a}_{half}", tag="back", bufs=2)
                for bb in range(2):
                    for u in range(2):
                        nc.tensor.transpose(back[:, bb, u, :], xt[a][:, 2 * half + bb, u, :], ident_f[:])
                cols = slice(2 * P * half, 2 * P * (half + 1))
                nc.scalar.copy(
                    out=xg[:, cols, :].rearrange("p (b j) u -> p b j u", b=2),
                    in_=back[:].rearrange("p b u j -> p b j u"),
                )
                nc.vector.quantize_mx(
                    out=codes[:, cols].bitcast(FP8X4), scales=scales[:, cols],
                    in_=xg[:, cols, :].rearrange("p j u -> p (j u)").bitcast(BF16),
                )
            xq[a] = (codes, scales)

        products(0)
        quantize_weights([(1, w1, P, P)], "second", nc.vector.tensor_copy)
        vec_turned = psum.tile([P, P], F32, name="vec_turned", tag="back", bufs=2)
        nc.tensor.transpose(vec_turned[:], vec_rows[:], ident_f[:])
        vec_cols = keep.tile([P, 2 * TILES], F32, name="vec_cols", tag="f0", align_bytes=64)
        nc.scalar.copy(out=vec_cols[:], in_=vec_turned[:, : 2 * TILES])
        def pick_into(c):
            if c == 0:
                pick(c, site_t[1])
            elif c == 5:
                pick(c, keep.tile([P, PICK], F32, name=f"picked{c}", tag="late5", align_bytes=64))
            else:
                pick(c, work.tile([P, PICK], F32, name=f"picked{c}", tag="picked", bufs=2))

        ahead = 3
        for c in range(TILES):
            h = work.tile([P, S], F32, name=f"h{c}", tag="h", bufs=1)
            if c < ahead:
                if c > 0:
                    products(c)
                    pick_into(c - 1)
                add_second(c, h)
                if c == ahead - 1:
                    products(c + 1)
                tie = f"f{c}"
            else:
                add_second_aside(c, h)
                if c + 1 < TILES:
                    products(c + 1)
                pick_into(c - 1)
                tie = f"site{c}"
            if c > 0:
                quantize_weights([pairs[c - 1]], tie, nc.scalar.copy)
            if c == TILES - 1:
                quantize_x(0, "xg0", "late5")
            put(c, h)
        pick_into(TILES - 1)

        shared = {}

        def pick_shared(n, tag):
            shared[n] = keep.tile([P, PICK], F32, name=f"shared{n}", tag=tag, align_bytes=64)
            nc.vector.tensor_copy(out=shared[n][:], in_=page[n][:].indirect(idx4[:]))

        for n in range(TILES - 2):
            pick_shared(n, f"site{n}" if n < ahead else f"f{n}")
        quantize_x(1, "page2", "xcodes1")
        pick_shared(TILES - 2, "page2")

        banks = [("y", 2), ("y", 2), ("p1", 2), ("p1", 2), ("p4", 1), ("turned", 1), ("back", 2), ("back", 2)]
        for n in range(TILES):
            tag, bufs = banks[n]
            y = psum.tile([P, PICK], F32, name=f"y{n}", tag=tag, bufs=bufs)
            for a in range(PASSES):
                codes, scales = quant[(3, n, a)]
                nc.tensor.matmul_mx(
                    out=y[:], lhsT=codes.bitcast(FP8X4), lhsT_scale=scales,
                    rhs=xq[a][0][:].bitcast(FP8X4), rhs_scale=xq[a][1][:], start=(a == 0), stop=(a == PASSES - 1),
                )
            if n == TILES - 1:
                pick_shared(n, "f5")
            parts = 2 if n == TILES - 1 else 1
            width = PICK // parts
            pending = []
            for part in range(parts):
                cols = slice(part * width, (part + 1) * width)
                upper = work.tile([P, width], F32, name=f"upper{n}_{part}", tag="upper", bufs=4)
                lower = work.tile([P, width], F32, name=f"lower{n}_{part}", tag="lower", bufs=4)
                nc.vector.scalar_tensor_tensor(
                    out=upper[:], in0=shared[n][:, cols], scalar=vec_cols[:, TILES + n : TILES + n + 1],
                    in1=y[:, cols], op0=ALU.mult, op1=ALU.max,
                )
                nc.vector.tensor_tensor(out=lower[:], in0=y[:, cols], in1=lim[n][:, cols], op=ALU.min)
                pending.append((cols, upper, lower))
            for cols, upper, lower in pending:
                adder = nc.gpsimd if n + 1 < TILES else nc.vector
                adder.tensor_tensor(out=lim[n][:, cols], in0=upper[:], in1=lower[:], op=ALU.add)
                nc.sync.dma_start(out=out[n * P : (n + 1) * P, cols], in_=lim[n][:, cols])
